import numpy as np
import ml_dtypes


def mxq(x, axis, fmt="e4m3"):
    dtype, down = {"e4m3": (ml_dtypes.float8_e4m3fn, 7), "e5m2": (ml_dtypes.float8_e5m2, 14)}[fmt]
    v = np.moveaxis(np.asarray(x, np.float32).astype(ml_dtypes.bfloat16).astype(np.float64), axis, -1)
    blocks = v.reshape(v.shape[:-1] + (-1, 32))
    amax = np.abs(blocks).max(-1, keepdims=True)
    byte = np.maximum(np.where(amax > 0, np.frexp(amax)[1] - 1 + 127, 0) - down, 1)
    scale = np.exp2(byte - 127.0)
    codes = (blocks / scale).astype(np.float32).astype(dtype).astype(np.float64)
    return np.moveaxis((codes * scale).reshape(v.shape), -1, axis)


WIDE = False


def mx_kscale(k):
    if not WIDE:
        return np.ones(k)
    levels = np.array([10, -10, 5, -5, 0])
    if k % 512:
        return np.exp2(np.random.permutation(np.resize(levels, k // 32))).repeat(32)
    a = np.empty((k // 512, 16))
    for p in range(k // 512):
        a[p, :8] = np.random.permutation(np.resize(levels, 8))
        for g in range(8):
            far = levels[np.abs(levels - a[p, g]) >= 10]
            a[p, g + 8] = far[np.random.randint(len(far))]
    return np.exp2(a.ravel()).repeat(32)


def f64(x):
    return np.asarray(x).astype(np.float64)


def striped(idx):
    return np.tile(idx.reshape(-1, 16).T, (8, 1)).astype(np.uint16)


def unstriped(offs):
    return offs[:16].T.reshape(-1).astype(np.int64)


E2M1 = np.array([0.0, 0.5, 1.0, 1.5, 2.0, 3.0, 4.0, 6.0, -0.0, -0.5, -1.0, -1.5, -2.0, -3.0, -4.0, -6.0])


def pack_weight(w, fmt):
    k, n = w.shape
    w = f64(np.asarray(w, np.float32).astype(ml_dtypes.bfloat16)).reshape(k // 32, 32, n)
    amax = np.abs(w).max(1)
    if fmt == "e4m3":
        byte = np.frexp(amax)[1] - 1 + 127 - 7
    else:
        mant, ex = np.frexp(amax / 6.0)
        byte = np.where(mant > 0.5, ex, ex - 1) + 127
    byte = np.clip(np.where(amax > 0, byte, 1), 1, 254)
    scaled = (w * np.exp2(127.0 - byte)[:, None, :]).reshape(k, n).astype(np.float32)
    by_word = np.ascontiguousarray(scaled.reshape(k // 512, 128, 4, n).transpose(0, 1, 3, 2))
    if fmt == "e4m3":
        words = by_word.astype(ml_dtypes.float8_e4m3fn).view(np.uint8)
    else:
        c = by_word.astype(ml_dtypes.float4_e2m1fn).view(np.uint8) & 0xF
        words = (c[..., 0::2] | (c[..., 1::2] << 4)).reshape(k // 512, 128, 2 * n)
    return np.ascontiguousarray(words), np.ascontiguousarray(byte.astype(np.uint8).reshape(k // 512, 16, n))


def unpack_weight(words, scales, fmt):
    g, _, n = scales.shape
    words = np.ascontiguousarray(words).reshape(g, 128, n, -1)
    if fmt == "e4m3":
        vals = words.view(ml_dtypes.float8_e4m3fn).astype(np.float64)
    else:
        nib = np.empty((g, 128, n, 4), np.uint8)
        nib[..., 0::2] = words & 0xF
        nib[..., 1::2] = words >> 4
        vals = E2M1[nib]
    vals = vals * np.repeat(np.exp2(scales.astype(np.float64) - 127.0), 8, axis=1)[..., None]
    return vals.transpose(0, 1, 3, 2).reshape(g * 512, n)


def gelu(v):
    return 0.5 * v * (1.0 + np.tanh(np.sqrt(2.0 / np.pi) * (v + 0.044715 * v**3)))


K, H, N, T, S, T2 = 1024, 512, 768, 4096, 1024, 2048

def setup_inputs():
    n = np.random.standard_normal
    s = mx_kscale(K)[:, None]
    u = mx_kscale(H)[:, None]
    tab_words, tab_scales = pack_weight(n((K, T)) * s, "e4m3")
    wb_words, wb_scales = pack_weight(0.55 * n((K, H)) / np.sqrt(K) / s, "e2m1")
    wd_words, wd_scales = pack_weight(0.8 * n((K, N)) / np.sqrt(K) / s, "e4m3")
    return {
        "tab_words": tab_words, "tab_scales": tab_scales,
        "offs": striped(np.random.permutation(T)[:S]),
        "offs2": striped(np.random.permutation(T)[:S]),
        "offs3": striped(np.random.permutation(T2)[:S]),
        "wa": (1.1 * n((K, H)) / np.sqrt(K) / s).astype(np.float32),
        "ba": (0.6 * n(H)).astype(np.float32),
        "wb_words": wb_words, "wb_scales": wb_scales,
        "gain": (np.exp(0.3 * n(H)) * u[:, 0]).astype(np.float32),
        "wc": (1.3 * n((H, N)) / np.sqrt(H) / u).astype(np.float32),
        "wd_words": wd_words, "wd_scales": wd_scales,
        "wgo": np.exp(0.3 * n((128, S))).astype(np.float32),
    }

def reference(tab_words, tab_scales, offs, offs2, offs3, wa, ba, wb_words, wb_scales, gain, wc, wd_words, wd_scales, wgo):
    TW = unpack_weight(tab_words, tab_scales, "e4m3")
    v = TW[:, unstriped(offs)]
    v2 = TW[:, unstriped(offs2)]
    ask = np.tanh((mxq(f64(wa), 0, "e4m3").T @ v) + f64(ba)[:, None])
    offer = np.sin(unpack_weight(wb_words, wb_scales, "e2m1").T @ v2)
    h = (ask + offer) * f64(gain)[:, None]
    fit = mxq(f64(wc), 0, "e4m3").T @ mxq(h, 0, "e4m3")
    own = unpack_weight(wd_words, wd_scales, "e4m3").T @ v2
    y = np.abs(np.maximum(fit, own))
    out = np.zeros((N, T2))
    out[:, unstriped(offs3)] = np.tile(f64(wgo), (N // 128, 1)) * y
    return out

@@ -1,0 +1,409 @@
+import math
+from contextlib import ExitStack
+
+import concourse.mybir as mybir
+from concourse.masks import make_identity
+
+K, H, N, T, S, T2 = 1024, 512, 768, 4096, 1024, 2048
+FLOPS = 2 * S * (2 * K * H + H * N + K * N)
+
+F32 = mybir.dt.float32
+BF16 = mybir.dt.bfloat16
+I32 = mybir.dt.int32
+U32 = mybir.dt.uint32
+U16 = mybir.dt.uint16
+U8 = mybir.dt.uint8
+FP8X4 = mybir.dt.float8_e4m3fn_x4
+FP4X4 = mybir.dt.float4_e2m1fn_x4
+ACT = mybir.ActivationFunctionType
+ALU = mybir.AluOpType
+
+P = 128
+PASSES = K // 512
+HALF = 512
+CHUNK = 256
+CHUNKS = S // CHUNK
+BANK = 512
+TILES = N // P
+EARLY = 256
+MAGIC = 1.5 * 2.0**23
+
+
+def tile_list_lesson_match_scores_kernel(
+    tc, tab_words, tab_scales, offs, offs2, offs3, wa, ba, wb_words, wb_scales, gain, wc, wd_words, wd_scales, wgo, out
+):
+    nc = tc.nc
+    with ExitStack() as ctx:
+        keep = ctx.enter_context(tc.tile_pool(name="keep", bufs=1))
+        work = ctx.enter_context(tc.tile_pool(name="work", bufs=2))
+        psum = ctx.enter_context(tc.psum_pool(name="psum", bufs=2))
+
+        def kept(name, shape, dtype, tag=""):
+            return keep.tile(shape, dtype, name=name, tag=tag, align_bytes=64)
+
+        pupil_list = kept("pupil_list", [P, S // 16], U16)
+        tutor_list = kept("tutor_list", [P, S // 16], U16)
+        place_list = kept("place_list", [P, S // 16], U16)
+
+        table = [kept("table%d" % a, [P, T], I32) for a in range(PASSES)]
+        table_scales = kept("table_scales", [P, T], U8)
+        pupil, tutor = {}, {}
+        pupil_scales = kept("pupil_scales", [P, S], U8)
+        tutor_scales = kept("tutor_scales", [P, S], U8)
+        tutor_scales1 = kept("tutor_scales1", [P, S], U8)
+
+        wa_raw = [kept("wa_raw%d" % a, [P, 4, H], F32, tag="wa_raw%d" % a) for a in range(PASSES)]
+        wa_codes = [kept("wa_codes%d" % a, [P, H], U32) for a in range(PASSES)]
+        wa_scales = [kept("wa_scales%d" % a, [P, H], U8) for a in range(PASSES)]
+        wb_codes = kept("wb_codes", [P, PASSES, 2 * H], U8)
+        wb_sc = kept("wb_sc", [P, PASSES, H], U8)
+        wd_codes = [kept("wd_codes0", [P, PASSES, EARLY], I32), kept("wd_codes1", [P, PASSES, N - EARLY], I32)]
+        wd_sc = kept("wd_sc", [P, PASSES, N], U8)
+        wc_raw = [kept("wc_raw0", [P, 4, EARLY], F32), kept("wc_raw1", [P, 4, N - EARLY], F32)]
+        wc_codes = kept("wc_codes", [P, N], U32)
+        wc_scales = kept("wc_scales", [P, N], U8)
+        h_codes = kept("h_codes", [P, S], U32)
+        h_scales = kept("h_scales", [P, S], U8)
+        weights = kept("weights", [P, S], F32)
+        rows = kept("rows", [P, P], F32)
+        identity = kept("identity", [P, P], F32)
+        columns = kept("columns", [P, 8], F32)
+        pages = [kept("page%d" % b, [P, T2], F32) for b in range(TILES)]
+
+        nc.gpsimd.memset(table_scales[:].bitcast(I32), 0)
+        nc.gpsimd.memset(wb_sc[:].bitcast(I32), 0)
+        nc.gpsimd.memset(tutor_scales1[:].bitcast(I32), 0)
+        nc.gpsimd.memset(wd_sc[:].bitcast(I32), 0)
+        nc.gpsimd.memset(rows[:], 0.0)
+        make_identity(nc, identity[:])
+        for page in pages:
+            for half in range(2):
+                nc.gpsimd.memset(page[:, T2 // 2 * half : T2 // 2 * (half + 1)], 0.0)
+
+        def load_scale_rows(tile, dram):
+            for q in range(4):
+                nc.sync.dma_start(
+                    tile[32 * q : 32 * q + 4, :, :].bitcast(I32),
+                    dram[:, 4 * q : 4 * q + 4, :].rearrange("a r n -> r a n").bitcast(I32),
+                )
+
+        def load_wd(s, n0, n1):
+            nc.sync.dma_start(
+                wd_codes[s][:], wd_words.rearrange("a p n i -> p a (n i)")[:, :, 4 * n0 : 4 * n1].bitcast(I32)
+            )
+
+        def load_wc(s, n0, n1):
+            by_plane = wc.rearrange("(g t i) n -> t g i n", t=4, i=8)
+            for t in range(4):
+                nc.sync.dma_start(wc_raw[s][:, t, :], by_plane[t][:, :, n0:n1])
+
+        def load_table(a):
+            nc.sync.dma_start(table[a][:], tab_words[a].rearrange("p t i -> p (t i)").bitcast(I32))
+
+        def load_wa(a):
+            nc.sync.dma_start(wa_raw[a][:], wa[512 * a : 512 * (a + 1), :].rearrange("(p j) c -> p j c", j=4))
+
+        nc.sync.dma_start(tutor_list[:], offs2)
+        nc.sync.dma_start(pupil_list[:], offs)
+        for q in range(4):
+            nc.sync.dma_start(
+                table_scales[32 * q : 32 * q + 8, :].bitcast(I32), tab_scales[:, 4 * q : 4 * q + 4, :].bitcast(I32)
+            )
+        load_table(0)
+        load_scale_rows(wb_sc, wb_scales)
+        load_table(1)
+        nc.sync.dma_start(wb_codes[:].bitcast(I32), wb_words.rearrange("a p b -> p a b").bitcast(I32))
+        load_wa(0)
+        nc.sync.dma_start(rows[0:4, :].rearrange("t (g i) -> t g i", i=8), ba.rearrange("(g t i) -> t g i", t=4, i=8))
+        nc.sync.dma_start(rows[4:8, :].rearrange("t (g i) -> t g i", i=8), gain.rearrange("(g t i) -> t g i", t=4, i=8))
+        load_wa(1)
+        load_wc(0, 0, EARLY)
+        load_wd(0, 0, EARLY)
+        load_scale_rows(wd_sc, wd_scales)
+        load_wc(1, EARLY, N)
+        load_wd(1, EARLY, N)
+        nc.sync.dma_start(place_list[:], offs3)
+        nc.sync.dma_start(weights[:], wgo)
+
+        def picked(words, a, j0, width):
+            return words[a, j0 // HALF][:, j0 % HALF : j0 % HALF + width].bitcast(FP8X4)
+
+        def gather_words(dst, a, lst, half, room):
+            dst[a, half] = room
+            nc.vector.tensor_copy(
+                room,
+                table[a][:].bitcast(U32).indirect(lst[:, 32 * half : 32 * (half + 1)]),
+            )
+
+        def quantise_wa_planes(a, b):
+            grouped = work.tile([P, 2, P, 4], BF16, name="wa_grouped", align_bytes=64)
+            for u in range(2):
+                nc.vector.tensor_copy(
+                    grouped[:, u].rearrange("p (g h i) j -> p g h j i", h=2, i=4),
+                    wa_raw[a][:].rearrange("p j (g t h i) -> p t g h j i", t=4, h=2, i=4)[:, 2 * b + u],
+                )
+            nc.vector.quantize_mx(
+                wa_codes[a][:, 2 * P * b : 2 * P * (b + 1)].bitcast(FP8X4),
+                wa_scales[a][:, 2 * P * b : 2 * P * (b + 1)],
+                grouped[:].rearrange("p u m j -> p (u m j)"),
+            )
+
+        def quantise_wc_pair(pair):
+            s, n0 = (0, 0) if pair == 0 else (1, 256 * pair - EARLY)
+            grouped = work.tile([P, 256, 4], BF16, name="wc_grouped", align_bytes=64)
+            nc.scalar.copy(
+                grouped[:].rearrange("p (c i) t -> p c t i", i=4),
+                wc_raw[s][:, :, n0 : n0 + 256].rearrange("p t (c i) -> p c t i", i=4),
+            )
+            nc.vector.quantize_mx(
+                wc_codes[:, 256 * pair : 256 * (pair + 1)].bitcast(FP8X4),
+                wc_scales[:, 256 * pair : 256 * (pair + 1)],
+                grouped[:].rearrange("p m j -> p (m j)"),
+            )
+
+        nc.vector.tensor_copy(tutor_scales[:], table_scales[:].indirect(tutor_list[:]))
+        nc.scalar.dma_start(tutor_scales1[0:64, :].bitcast(I32), tutor_scales[4:68, :].bitcast(I32))
+        nc.scalar.dma_start(tutor_scales1[64:100, :].bitcast(I32), tutor_scales[68:104, :].bitcast(I32))
+        nc.vector.tensor_copy(pupil_scales[:], table_scales[:].indirect(pupil_list[:]))
+        gather_words(tutor, 0, tutor_list, 0, kept("tutor00", [P, HALF], U32)[:])
+        gather_words(pupil, 0, pupil_list, 0, kept("pupil00", [P, HALF], U32)[:])
+        gather_words(tutor, 0, tutor_list, 1, kept("tutor01", [P, HALF], U32)[:])
+        gather_words(pupil, 0, pupil_list, 1, kept("pupil01", [P, HALF], U32)[:])
+        gather_words(tutor, 1, tutor_list, 0, kept("tutor10", [P, HALF], U32)[:])
+        gather_words(pupil, 1, pupil_list, 0, kept("pupil10", [P, HALF], U32)[:])
+        gather_words(pupil, 1, pupil_list, 1, kept("pupil11", [P, HALF], U32)[:])
+        turned = psum.tile([P, BANK], F32, name="fit")
+        nc.tensor.transpose(turned[:, 0:P], rows[:], identity[:])
+        nc.scalar.copy(columns[:], turned[:, 0:8])
+
+        tutor_plane = [tutor_scales[:], tutor_scales1[:]]
+        pupil_plane = [pupil_scales[:], pupil_scales[4:P, :]]
+
+        fractions, turns, sines, tanhs, sums = {}, {}, {}, {}, {}
+
+        def offer_product(c, b):
+            if b == 0:
+                fractions[c] = kept("revolutions", [P, 2, H], F32, tag="sine_terms")
+            revolutions = fractions[c]
+            cols = slice(CHUNK * c + P * b, CHUNK * c + P * (b + 1))
+            bank = psum.tile([P, BANK], F32, name="stage", bufs=4)
+            for a in range(PASSES):
+                nc.tensor.matmul_mx(
+                    bank[:],
+                    lhsT=picked(tutor, a, cols.start, P),
+                    lhsT_scale=tutor_plane[a][:, cols],
+                    rhs=wb_codes[:, a, :].bitcast(FP4X4),
+                    rhs_scale=wb_sc[:, a, :],
+                    start=(a == 0),
+                    stop=(a == PASSES - 1),
+                )
+            by_plane = bank[:].rearrange("p (g t i) -> p t g i", t=4, i=8)
+            shifted = kept("shifted", [P, H], U32, tag="phase%d" % b)
+            nc.scalar.activation(
+                shifted[:].rearrange("p (t g i) -> p t g i", t=4, i=8),
+                by_plane,
+                ACT.Silu,
+                bias=MAGIC,
+                scale=1.0 / (2.0 * math.pi),
+            )
+            nc.scalar.activation(
+                revolutions[:, b, :].rearrange("p (t g i) -> p t g i", t=4, i=8),
+                by_plane,
+                ACT.Copy,
+                scale=1.0 / (2.0 * math.pi),
+            )
+            whole = work.tile([P, H], F32, name="whole")
+            nc.scalar.activation(whole[:], shifted[:], ACT.Copy, bias=MAGIC, scale=-1.0)
+            turns[c, b] = (revolutions[:, b, :], whole[:])
+
+        def offer_sine(c):
+            angles = [psum.tile([P, BANK], F32, name="stage", bufs=4) for b in range(2)]
+            for jt in range(2):
+                for t in range(4):
+                    at = CHUNK * (t % 2) + P * jt
+                    for term in range(2):
+                        nc.tensor.matmul(
+                            angles[t // 2][:, at : at + P],
+                            lhsT=turns[c, jt][term][:, P * t : P * (t + 1)],
+                            rhs=identity[:],
+                            is_transpose=True,
+                            start=(term == 0),
+                            stop=(term == 1),
+                        )
+            plain = [kept("sine", [P, BANK], F32, tag="phase%d" % b) for b in range(2)]
+            for b in range(2):
+                nc.scalar.activation(plain[b][:], angles[b][:], ACT.Sin, scale=2.0 * math.pi)
+            gained = kept("gained", [P, 4, CHUNK], F32, tag="sine_terms")
+            for t in range(4):
+                sine = plain[t // 2][:, CHUNK * (t % 2) : CHUNK * (t % 2 + 1)]
+                if c == 0:
+                    nc.vector.tensor_scalar(gained[:, t, :], sine, columns[:, 4 + t : 5 + t], None, ALU.mult)
+                else:
+                    nc.scalar.activation(gained[:, t, :], sine, ACT.Copy, scale=columns[:, 4 + t : 5 + t])
+                sines[c, t] = gained[:, t, :]
+
+        def ask_product(c):
+            cols = slice(CHUNK * c, CHUNK * (c + 1))
+            for b in range(2):
+                bank = psum.tile([P, BANK], F32, name="stage", bufs=4)
+                for u in range(2):
+                    t = 2 * b + u
+                    for a in range(PASSES):
+                        nc.tensor.matmul_mx(
+                            bank[:, CHUNK * u : CHUNK * (u + 1)],
+                            lhsT=wa_codes[a][:, P * t : P * (t + 1)].bitcast(FP8X4),
+                            lhsT_scale=wa_scales[a][:, P * t : P * (t + 1)],
+                            rhs=picked(pupil, a, cols.start, CHUNK),
+                            rhs_scale=pupil_plane[a][:, cols],
+                            start=(a == 0),
+                            stop=(a == PASSES - 1),
+                        )
+                for u in range(2):
+                    t = 2 * b + u
+                    ask = work.tile([P, CHUNK], F32, name="ask_sb", bufs=4)
+                    nc.scalar.activation(
+                        ask[:], bank[:, CHUNK * u : CHUNK * (u + 1)], ACT.Tanh, bias=columns[:, t : t + 1]
+                    )
+                    tanhs[c, t] = ask
+
+        def add_up(c):
+            total = kept("total", [P, 4, CHUNK], F32, tag="total")
+            for t in range(4):
+                nc.vector.scalar_tensor_tensor(
+                    total[:, t, :], tanhs[c, t][:], columns[:, 4 + t : 5 + t], sines[c, t], ALU.mult, ALU.add
+                )
+            sums[c] = total
+
+        grouped_h = {}
+
+        def interleave_h(c, engine_copy, grouped):
+            engine_copy(
+                grouped[:].rearrange("p (c i) t -> p c t i", i=4), sums[c][:].rearrange("p t (c i) -> p c t i", i=4)
+            )
+            grouped_h[c] = grouped
+
+        def quantise_h(c):
+            cols = slice(CHUNK * c, CHUNK * (c + 1))
+            nc.vector.quantize_mx(
+                h_codes[:, cols].bitcast(FP8X4), h_scales[:, cols], grouped_h[c][:].rearrange("p m j -> p (m j)")
+            )
+
+        owns, maxima, scores = {}, {}, {}
+
+        def own_product(cell):
+            bank = psum.tile([P, BANK], F32, name="own")
+            at = 0
+            for tile, j0, width in cell:
+                s, n0 = (0, P * tile) if P * tile < EARLY else (1, P * tile - EARLY)
+                for a in range(PASSES):
+                    nc.tensor.matmul_mx(
+                        bank[:, at : at + width],
+                        lhsT=wd_codes[s][:, a, n0 : n0 + P].bitcast(FP8X4),
+                        lhsT_scale=wd_sc[:, a, P * tile : P * (tile + 1)],
+                        rhs=picked(tutor, a, j0, width),
+                        rhs_scale=tutor_plane[a][:, j0 : j0 + width],
+                        start=(a == 0),
+                        stop=(a == PASSES - 1),
+                    )
+                at += width
+            own = work.tile([P, BANK], F32, name="own_sb", bufs=5)
+            nc.scalar.copy(own[:, 0:at], bank[:, 0:at])
+            owns[cell] = own
+
+        def score(cell):
+            bank = psum.tile([P, BANK], F32, name="fit")
+            at = 0
+            for tile, j0, width in cell:
+                nc.tensor.matmul_mx(
+                    bank[:, at : at + width],
+                    lhsT=wc_codes[:, P * tile : P * (tile + 1)].bitcast(FP8X4),
+                    lhsT_scale=wc_scales[:, P * tile : P * (tile + 1)],
+                    rhs=h_codes[:, j0 : j0 + width].bitcast(FP8X4),
+                    rhs_scale=h_scales[:, j0 : j0 + width],
+                    start=True,
+                    stop=True,
+                )
+                at += width
+            larger = work.tile([P, BANK], F32, name="larger", bufs=4)
+            nc.vector.tensor_tensor(larger[:, 0:at], bank[:, 0:at], owns[cell][:, 0:at], ALU.max)
+            maxima[cell] = larger
+
+        def magnitude(cell, first, count, size=None):
+            width = cell[0][2]
+            if size is None:
+                size = work.tile([P, BANK], F32, name="size", bufs=4)
+            nc.scalar.activation(
+                size[:, 0 : width * count], maxima[cell][:, width * first : width * (first + count)], ACT.Abs
+            )
+            for piece in range(count):
+                scores[cell, first + piece] = size[:, width * piece : width * (piece + 1)]
+
+        def place(cell, piece):
+            tile, j0, width = cell[piece]
+            page = pages[tile]
+            nc.vector.tensor_tensor(
+                page[:].indirect(place_list[:, j0 // 16 : (j0 + width) // 16]),
+                scores[cell, piece],
+                weights[:, j0 : j0 + width],
+                ALU.mult,
+            )
+            if j0 + width == S:
+                nc.sync.dma_start(out[P * tile : P * (tile + 1), :], page[:])
+
+        def narrow(c, *tiles):
+            return tuple((tile, CHUNK * c, CHUNK) for tile in tiles)
+
+        windows = [[narrow(c, 0, 1), narrow(c, 2, 3), narrow(c, 4, 5)] for c in range(2)]
+        windows.append([narrow(2, 0, 1), narrow(2, 4), narrow(2, 2, 3)])
+        windows.append([narrow(3, 0, 1), narrow(3, 2, 3), narrow(3, 4), ((5, HALF, HALF),)])
+
+        offer_product(0, 0)
+        offer_product(0, 1)
+        for a in range(PASSES):
+            for b in range(2):
+                quantise_wa_planes(a, b)
+        offer_sine(0)
+        ask_product(0)
+        quantise_wc_pair(0)
+        own_product(windows[0][0])
+        add_up(0)
+        interleave_h(0, nc.vector.tensor_copy, kept("h_grouped0", [P, CHUNK, 4], BF16, tag="first_h"))
+        quantise_h(0)
+        gather_words(tutor, 1, tutor_list, 1, kept("tutor11", [P, HALF], U32, tag="first_h")[:])
+        quantise_wc_pair(1)
+        own_product(windows[0][1])
+        for c in range(CHUNKS - 1):
+            first, second, third = windows[c]
+            score(first)
+            score(second)
+            if c > 0:
+                offer_product(c + 1, 0)
+            magnitude(first, 0, len(first))
+            if c == 0:
+                offer_product(c + 1, 0)
+                quantise_wc_pair(2)
+            offer_product(c + 1, 1)
+            magnitude(second, 0, len(second))
+            own_product(third)
+            for piece in range(len(first)):
+                place(first, piece)
+            score(third)
+            for piece in range(len(second)):
+                place(second, piece)
+            ask_product(c + 1)
+            offer_sine(c + 1)
+            add_up(c + 1)
+            magnitude(third, 0, 1)
+            interleave_h(c + 1, nc.scalar.copy, kept("h_grouped", [P, CHUNK, 4], BF16))
+            place(third, 0)
+            quantise_h(c + 1)
+            magnitude(third, 1, 1, kept("last_size", [P, CHUNK], F32, tag="total"))
+            for cell in windows[c + 1][: 2 if c + 2 < CHUNKS else 4]:
+                own_product(cell)
+            place(third, 1)
+        for cell in windows[-1]:
+            score(cell)
+            magnitude(cell, 0, len(cell))
+        for cell in windows[-1]:
+            for piece in range(len(cell)):
+                place(cell, piece)

@@ -25,7 +25,8 @@ CHUNK = 256
 CHUNKS = S // CHUNK
 BANK = 512
 TILES = N // P
-EARLY = 256
+RESIDENT = TILES - 1
+EARLY = 3 * P
 MAGIC = 1.5 * 2.0**23
 
 
@@ -45,7 +46,7 @@ def tile_list_lesson_match_scores_kernel(
         tutor_list = kept("tutor_list", [P, S // 16], U16)
         place_list = kept("place_list", [P, S // 16], U16)
 
-        table = [kept("table%d" % a, [P, T], I32) for a in range(PASSES)]
+        table = [kept("table%d" % a, [P, T], I32, tag="table%d" % a) for a in range(PASSES)]
         table_scales = kept("table_scales", [P, T], U8)
         pupil, tutor = {}, {}
         pupil_scales = kept("pupil_scales", [P, S], U8)
@@ -68,17 +69,21 @@ def tile_list_lesson_match_scores_kernel(
         rows = kept("rows", [P, P], F32)
         identity = kept("identity", [P, P], F32)
         columns = kept("columns", [P, 8], F32)
-        pages = [kept("page%d" % b, [P, T2], F32) for b in range(TILES)]
+        pages = {}
 
         nc.gpsimd.memset(table_scales[:].bitcast(I32), 0)
-        nc.gpsimd.memset(wb_sc[:].bitcast(I32), 0)
-        nc.gpsimd.memset(tutor_scales1[:].bitcast(I32), 0)
-        nc.gpsimd.memset(wd_sc[:].bitcast(I32), 0)
-        nc.gpsimd.memset(rows[:], 0.0)
         make_identity(nc, identity[:])
-        for page in pages:
-            for half in range(2):
-                nc.gpsimd.memset(page[:, T2 // 2 * half : T2 // 2 * (half + 1)], 0.0)
+        nc.vector.memset(wb_sc[:].bitcast(I32), 0)
+        nc.vector.memset(tutor_scales1[:].bitcast(I32), 0)
+        nc.vector.memset(wd_sc[:].bitcast(I32), 0)
+        nc.vector.memset(rows[:], 0.0)
+
+        def clear_page(tile, tag):
+            pages[tile] = kept("page%d" % tile, [P, T2], F32, tag=tag)
+            nc.vector.memset(pages[tile][:], 0.0)
+
+        for tile in range(3):
+            clear_page(tile, "")
 
         def load_scale_rows(tile, dram):
             for q in range(4):
@@ -148,16 +153,16 @@ def tile_list_lesson_match_scores_kernel(
                 grouped[:].rearrange("p u m j -> p (u m j)"),
             )
 
-        def quantise_wc_pair(pair):
-            s, n0 = (0, 0) if pair == 0 else (1, 256 * pair - EARLY)
-            grouped = work.tile([P, 256, 4], BF16, name="wc_grouped", align_bytes=64)
+        def quantise_wc(n0, width):
+            s, at = (0, n0) if n0 < EARLY else (1, n0 - EARLY)
+            grouped = work.tile([P, width, 4], BF16, name="wc_grouped", align_bytes=64)
             nc.scalar.copy(
                 grouped[:].rearrange("p (c i) t -> p c t i", i=4),
-                wc_raw[s][:, :, n0 : n0 + 256].rearrange("p t (c i) -> p c t i", i=4),
+                wc_raw[s][:, :, at : at + width].rearrange("p t (c i) -> p c t i", i=4),
             )
             nc.vector.quantize_mx(
-                wc_codes[:, 256 * pair : 256 * (pair + 1)].bitcast(FP8X4),
-                wc_scales[:, 256 * pair : 256 * (pair + 1)],
+                wc_codes[:, n0 : n0 + width].bitcast(FP8X4),
+                wc_scales[:, n0 : n0 + width],
                 grouped[:].rearrange("p m j -> p (m j)"),
             )
 
@@ -290,7 +295,7 @@ def tile_list_lesson_match_scores_kernel(
 
         owns, maxima, scores = {}, {}, {}
 
-        def own_product(cell):
+        def own_product(cell, own=None):
             bank = psum.tile([P, BANK], F32, name="own")
             at = 0
             for tile, j0, width in cell:
@@ -306,7 +311,8 @@ def tile_list_lesson_match_scores_kernel(
                         stop=(a == PASSES - 1),
                     )
                 at += width
-            own = work.tile([P, BANK], F32, name="own_sb", bufs=5)
+            if own is None:
+                own = work.tile([P, BANK], F32, name="own_sb", bufs=5)
             nc.scalar.copy(own[:, 0:at], bank[:, 0:at])
             owns[cell] = own
 
@@ -324,7 +330,7 @@ def tile_list_lesson_match_scores_kernel(
                     stop=True,
                 )
                 at += width
-            larger = work.tile([P, BANK], F32, name="larger", bufs=4)
+            larger = work.tile([P, BANK], F32, name="larger", bufs=5)
             nc.vector.tensor_tensor(larger[:, 0:at], bank[:, 0:at], owns[cell][:, 0:at], ALU.max)
             maxima[cell] = larger
 
@@ -353,9 +359,8 @@ def tile_list_lesson_match_scores_kernel(
         def narrow(c, *tiles):
             return tuple((tile, CHUNK * c, CHUNK) for tile in tiles)
 
-        windows = [[narrow(c, 0, 1), narrow(c, 2, 3), narrow(c, 4, 5)] for c in range(2)]
-        windows.append([narrow(2, 0, 1), narrow(2, 4), narrow(2, 2, 3)])
-        windows.append([narrow(3, 0, 1), narrow(3, 2, 3), narrow(3, 4), ((5, HALF, HALF),)])
+        windows = [[narrow(c, 0), narrow(c, 1, 2), narrow(c, 3, 4)] for c in range(CHUNKS)]
+        closing = [((5, HALF * half, HALF),) for half in range(2)]
 
         offer_product(0, 0)
         offer_product(0, 1)
@@ -364,13 +369,13 @@ def tile_list_lesson_match_scores_kernel(
                 quantise_wa_planes(a, b)
         offer_sine(0)
         ask_product(0)
-        quantise_wc_pair(0)
-        own_product(windows[0][0])
+        quantise_wc(0, P)
+        own_product(windows[0][0], kept("first_own", [P, BANK], F32, tag="page3"))
         add_up(0)
         interleave_h(0, nc.vector.tensor_copy, kept("h_grouped0", [P, CHUNK, 4], BF16, tag="first_h"))
         quantise_h(0)
         gather_words(tutor, 1, tutor_list, 1, kept("tutor11", [P, HALF], U32, tag="first_h")[:])
-        quantise_wc_pair(1)
+        quantise_wc(P, 2 * P)
         own_product(windows[0][1])
         for c in range(CHUNKS - 1):
             first, second, third = windows[c]
@@ -378,15 +383,18 @@ def tile_list_lesson_match_scores_kernel(
             score(second)
             if c > 0:
                 offer_product(c + 1, 0)
-            magnitude(first, 0, len(first))
+            magnitude(first, 0, len(first), kept("first_size", [P, BANK], F32, tag="page4") if c == 0 else None)
             if c == 0:
+                clear_page(3, "page3")
                 offer_product(c + 1, 0)
-                quantise_wc_pair(2)
-            offer_product(c + 1, 1)
+                quantise_wc(3 * P, 2 * P)
             magnitude(second, 0, len(second))
+            offer_product(c + 1, 1)
             own_product(third)
             for piece in range(len(first)):
                 place(first, piece)
+            if c == 0:
+                clear_page(4, "page4")
             score(third)
             for piece in range(len(second)):
                 place(second, piece)
@@ -394,16 +402,25 @@ def tile_list_lesson_match_scores_kernel(
             offer_sine(c + 1)
             add_up(c + 1)
             magnitude(third, 0, 1)
+            for cell in windows[c + 1][:2]:
+                own_product(cell)
             interleave_h(c + 1, nc.scalar.copy, kept("h_grouped", [P, CHUNK, 4], BF16))
             place(third, 0)
             quantise_h(c + 1)
-            magnitude(third, 1, 1, kept("last_size", [P, CHUNK], F32, tag="total"))
-            for cell in windows[c + 1][: 2 if c + 2 < CHUNKS else 4]:
-                own_product(cell)
+            magnitude(third, 1, 1)
             place(third, 1)
+        quantise_wc(5 * P, P)
+        for cell in windows[-1][2:] + closing:
+            own_product(cell)
         for cell in windows[-1]:
             score(cell)
             magnitude(cell, 0, len(cell))
+        closing_size = kept("closing_size", [P, S], F32)
+        for half, cell in enumerate(closing):
+            score(cell)
+            magnitude(cell, 0, 1, closing_size[:, HALF * half : HALF * (half + 1)])
         for cell in windows[-1]:
             for piece in range(len(cell)):
                 place(cell, piece)
+        nc.vector.tensor_tensor(pages[0][:].indirect(place_list[:]), closing_size[:], weights[:], ALU.mult)
+        nc.sync.dma_start(out[P * RESIDENT :, :], pages[0][:])

@@ -47,7 +47,7 @@ def tile_list_lesson_match_scores_kernel(
         place_list = kept("place_list", [P, S // 16], U16)
 
         table = [kept("table%d" % a, [P, T], I32, tag="table%d" % a) for a in range(PASSES)]
-        table_scales = kept("table_scales", [P, T], U8)
+        table_scales = kept("table_scales", [P, T], U8, tag="table_scales")
         pupil, tutor = {}, {}
         pupil_scales = kept("pupil_scales", [P, S], U8)
         tutor_scales = kept("tutor_scales", [P, S], U8)
@@ -78,12 +78,12 @@ def tile_list_lesson_match_scores_kernel(
         nc.vector.memset(wd_sc[:].bitcast(I32), 0)
         nc.vector.memset(rows[:], 0.0)
 
-        def clear_page(tile, tag):
+        def clear_page(tile, engine, tag):
             pages[tile] = kept("page%d" % tile, [P, T2], F32, tag=tag)
-            nc.vector.memset(pages[tile][:], 0.0)
+            engine.memset(pages[tile][:], 0.0)
 
         for tile in range(3):
-            clear_page(tile, "")
+            clear_page(tile, nc.vector, "")
 
         def load_scale_rows(tile, dram):
             for q in range(4):
@@ -153,10 +153,10 @@ def tile_list_lesson_match_scores_kernel(
                 grouped[:].rearrange("p u m j -> p (u m j)"),
             )
 
-        def quantise_wc(n0, width):
+        def quantise_wc(n0, width, tag, engine_copy=nc.scalar.copy):
             s, at = (0, n0) if n0 < EARLY else (1, n0 - EARLY)
-            grouped = work.tile([P, width, 4], BF16, name="wc_grouped", align_bytes=64)
-            nc.scalar.copy(
+            grouped = kept("wc_grouped", [P, width, 4], BF16, tag=tag)
+            engine_copy(
                 grouped[:].rearrange("p (c i) t -> p c t i", i=4),
                 wc_raw[s][:, :, at : at + width].rearrange("p t (c i) -> p c t i", i=4),
             )
@@ -170,13 +170,14 @@ def tile_list_lesson_match_scores_kernel(
         nc.scalar.dma_start(tutor_scales1[0:64, :].bitcast(I32), tutor_scales[4:68, :].bitcast(I32))
         nc.scalar.dma_start(tutor_scales1[64:100, :].bitcast(I32), tutor_scales[68:104, :].bitcast(I32))
         nc.vector.tensor_copy(pupil_scales[:], table_scales[:].indirect(pupil_list[:]))
+        clear_page(3, nc.gpsimd, "table_scales")
         gather_words(tutor, 0, tutor_list, 0, kept("tutor00", [P, HALF], U32)[:])
         gather_words(pupil, 0, pupil_list, 0, kept("pupil00", [P, HALF], U32)[:])
         gather_words(tutor, 0, tutor_list, 1, kept("tutor01", [P, HALF], U32)[:])
         gather_words(pupil, 0, pupil_list, 1, kept("pupil01", [P, HALF], U32)[:])
+        clear_page(4, nc.gpsimd, "table0")
         gather_words(tutor, 1, tutor_list, 0, kept("tutor10", [P, HALF], U32)[:])
         gather_words(pupil, 1, pupil_list, 0, kept("pupil10", [P, HALF], U32)[:])
-        gather_words(pupil, 1, pupil_list, 1, kept("pupil11", [P, HALF], U32)[:])
         turned = psum.tile([P, BANK], F32, name="fit")
         nc.tensor.transpose(turned[:, 0:P], rows[:], identity[:])
         nc.scalar.copy(columns[:], turned[:, 0:8])
@@ -184,12 +185,9 @@ def tile_list_lesson_match_scores_kernel(
         tutor_plane = [tutor_scales[:], tutor_scales1[:]]
         pupil_plane = [pupil_scales[:], pupil_scales[4:P, :]]
 
-        fractions, turns, sines, tanhs, sums = {}, {}, {}, {}, {}
+        offers, fractions, turns, sines, tanhs, sums = {}, {}, {}, {}, {}, {}
 
         def offer_product(c, b):
-            if b == 0:
-                fractions[c] = kept("revolutions", [P, 2, H], F32, tag="sine_terms")
-            revolutions = fractions[c]
             cols = slice(CHUNK * c + P * b, CHUNK * c + P * (b + 1))
             bank = psum.tile([P, BANK], F32, name="stage", bufs=4)
             for a in range(PASSES):
@@ -211,6 +209,13 @@ def tile_list_lesson_match_scores_kernel(
                 bias=MAGIC,
                 scale=1.0 / (2.0 * math.pi),
             )
+            offers[c, b] = (by_plane, shifted)
+
+        def offer_turns(c, b):
+            by_plane, shifted = offers[c, b]
+            if b == 0:
+                fractions[c] = kept("revolutions", [P, 2, H], F32, tag="sine_terms")
+            revolutions = fractions[c]
             nc.scalar.activation(
                 revolutions[:, b, :].rearrange("p (t g i) -> p t g i", t=4, i=8),
                 by_plane,
@@ -362,55 +367,60 @@ def tile_list_lesson_match_scores_kernel(
         windows = [[narrow(c, 0), narrow(c, 1, 2), narrow(c, 3, 4)] for c in range(CHUNKS)]
         closing = [((5, HALF * half, HALF),) for half in range(2)]
 
-        offer_product(0, 0)
-        offer_product(0, 1)
+        for b in range(2):
+            offer_product(0, b)
+            offer_turns(0, b)
         for a in range(PASSES):
             for b in range(2):
                 quantise_wa_planes(a, b)
+        gather_words(pupil, 1, pupil_list, 1, kept("pupil11", [P, HALF], U32, tag="wa_raw1")[:])
         offer_sine(0)
         ask_product(0)
-        quantise_wc(0, P)
-        own_product(windows[0][0], kept("first_own", [P, BANK], F32, tag="page3"))
+        quantise_wc(0, P, "")
+        own_product(windows[0][0])
         add_up(0)
         interleave_h(0, nc.vector.tensor_copy, kept("h_grouped0", [P, CHUNK, 4], BF16, tag="first_h"))
         quantise_h(0)
         gather_words(tutor, 1, tutor_list, 1, kept("tutor11", [P, HALF], U32, tag="first_h")[:])
-        quantise_wc(P, 2 * P)
+        quantise_wc(P, 2 * P, "phase0")
         own_product(windows[0][1])
         for c in range(CHUNKS - 1):
             first, second, third = windows[c]
             score(first)
             score(second)
             if c > 0:
-                offer_product(c + 1, 0)
-            magnitude(first, 0, len(first), kept("first_size", [P, BANK], F32, tag="page4") if c == 0 else None)
+                offer_turns(c + 1, 0)
+            magnitude(first, 0, len(first))
             if c == 0:
-                clear_page(3, "page3")
                 offer_product(c + 1, 0)
-                quantise_wc(3 * P, 2 * P)
+                offer_turns(c + 1, 0)
+                quantise_wc(3 * P, 2 * P, "wc34", nc.vector.tensor_copy)
             magnitude(second, 0, len(second))
             offer_product(c + 1, 1)
+            offer_turns(c + 1, 1)
             own_product(third)
             for piece in range(len(first)):
                 place(first, piece)
-            if c == 0:
-                clear_page(4, "page4")
             score(third)
             for piece in range(len(second)):
                 place(second, piece)
             ask_product(c + 1)
             offer_sine(c + 1)
             add_up(c + 1)
-            magnitude(third, 0, 1)
+            magnitude(third, 0, 1, kept("held_size0", [P, CHUNK], F32, tag="phase1"))
             for cell in windows[c + 1][:2]:
                 own_product(cell)
+            if c + 2 < CHUNKS:
+                offer_product(c + 2, 0)
+            else:
+                own_product(windows[c + 1][2])
             interleave_h(c + 1, nc.scalar.copy, kept("h_grouped", [P, CHUNK, 4], BF16))
             place(third, 0)
             quantise_h(c + 1)
             magnitude(third, 1, 1)
             place(third, 1)
-        quantise_wc(5 * P, P)
-        for cell in windows[-1][2:] + closing:
+        quantise_wc(5 * P, P, "")
+        for cell in closing:
             own_product(cell)
         for cell in windows[-1]:
             score(cell)

import math
from contextlib import ExitStack

import concourse.mybir as mybir
from concourse.masks import make_identity

K, H, N, T, S, T2 = 1024, 512, 768, 4096, 1024, 2048
FLOPS = 2 * S * (2 * K * H + H * N + K * N)

F32 = mybir.dt.float32
BF16 = mybir.dt.bfloat16
I32 = mybir.dt.int32
U32 = mybir.dt.uint32
U16 = mybir.dt.uint16
U8 = mybir.dt.uint8
FP8X4 = mybir.dt.float8_e4m3fn_x4
FP4X4 = mybir.dt.float4_e2m1fn_x4
ACT = mybir.ActivationFunctionType
ALU = mybir.AluOpType

P = 128
PASSES = K // 512
HALF = 512
CHUNK = 256
CHUNKS = S // CHUNK
BANK = 512
TILES = N // P
RESIDENT = TILES - 1
EARLY = 3 * P
MAGIC = 1.5 * 2.0**23


def tile_list_lesson_match_scores_kernel(
    tc, tab_words, tab_scales, offs, offs2, offs3, wa, ba, wb_words, wb_scales, gain, wc, wd_words, wd_scales, wgo, out
):
    nc = tc.nc
    with ExitStack() as ctx:
        keep = ctx.enter_context(tc.tile_pool(name="keep", bufs=1))
        work = ctx.enter_context(tc.tile_pool(name="work", bufs=2))
        psum = ctx.enter_context(tc.psum_pool(name="psum", bufs=2))

        def kept(name, shape, dtype, tag=""):
            return keep.tile(shape, dtype, name=name, tag=tag, align_bytes=64)

        pupil_list = kept("pupil_list", [P, S // 16], U16)
        tutor_list = kept("tutor_list", [P, S // 16], U16)
        place_list = kept("place_list", [P, S // 16], U16)

        table = [kept("table%d" % a, [P, T], I32, tag="table%d" % a) for a in range(PASSES)]
        table_scales = kept("table_scales", [P, T], U8, tag="table_scales")
        pupil, tutor = {}, {}
        pupil_scales = kept("pupil_scales", [P, S], U8)
        tutor_scales = kept("tutor_scales", [P, S], U8)
        tutor_scales1 = kept("tutor_scales1", [P, S], U8)

        wa_raw = [kept("wa_raw%d" % a, [P, 4, H], F32, tag="wa_raw%d" % a) for a in range(PASSES)]
        wa_codes = [kept("wa_codes%d" % a, [P, H], U32) for a in range(PASSES)]
        wa_scales = [kept("wa_scales%d" % a, [P, H], U8) for a in range(PASSES)]
        wb_codes = kept("wb_codes", [P, PASSES, 2 * H], U8)
        wb_sc = kept("wb_sc", [P, PASSES, H], U8)
        wd_codes = [kept("wd_codes0", [P, PASSES, EARLY], I32), kept("wd_codes1", [P, PASSES, N - EARLY], I32)]
        wd_sc = kept("wd_sc", [P, PASSES, N], U8)
        wc_raw = [kept("wc_raw0", [P, 4, EARLY], F32), kept("wc_raw1", [P, 4, N - EARLY], F32)]
        wc_codes = kept("wc_codes", [P, N], U32)
        wc_scales = kept("wc_scales", [P, N], U8)
        h_codes = kept("h_codes", [P, S], U32)
        h_scales = kept("h_scales", [P, S], U8)
        weights = kept("weights", [P, S], F32)
        rows = kept("rows", [P, P], F32)
        identity = kept("identity", [P, P], F32)
        columns = kept("columns", [P, 8], F32)
        pages = {}

        nc.gpsimd.memset(table_scales[:].bitcast(I32), 0)
        make_identity(nc, identity[:])
        nc.vector.memset(wb_sc[:].bitcast(I32), 0)
        nc.vector.memset(tutor_scales1[:].bitcast(I32), 0)
        nc.vector.memset(wd_sc[:].bitcast(I32), 0)
        nc.vector.memset(rows[:], 0.0)

        def clear_page(tile, engine, tag):
            pages[tile] = kept("page%d" % tile, [P, T2], F32, tag=tag)
            engine.memset(pages[tile][:], 0.0)

        for tile in range(3):
            clear_page(tile, nc.vector, "")

        def load_scale_rows(tile, dram):
            for q in range(4):
                nc.sync.dma_start(
                    tile[32 * q : 32 * q + 4, :, :].bitcast(I32),
                    dram[:, 4 * q : 4 * q + 4, :].rearrange("a r n -> r a n").bitcast(I32),
                )

        def load_wd(s, n0, n1):
            nc.sync.dma_start(
                wd_codes[s][:], wd_words.rearrange("a p n i -> p a (n i)")[:, :, 4 * n0 : 4 * n1].bitcast(I32)
            )

        def load_wc(s, n0, n1):
            by_plane = wc.rearrange("(g t i) n -> t g i n", t=4, i=8)
            for t in range(4):
                nc.sync.dma_start(wc_raw[s][:, t, :], by_plane[t][:, :, n0:n1])

        def load_table(a):
            nc.sync.dma_start(table[a][:], tab_words[a].rearrange("p t i -> p (t i)").bitcast(I32))

        def load_wa(a):
            nc.sync.dma_start(wa_raw[a][:], wa[512 * a : 512 * (a + 1), :].rearrange("(p j) c -> p j c", j=4))

        nc.sync.dma_start(tutor_list[:], offs2)
        nc.sync.dma_start(pupil_list[:], offs)
        for q in range(4):
            nc.sync.dma_start(
                table_scales[32 * q : 32 * q + 8, :].bitcast(I32), tab_scales[:, 4 * q : 4 * q + 4, :].bitcast(I32)
            )
        load_table(0)
        load_scale_rows(wb_sc, wb_scales)
        load_table(1)
        nc.sync.dma_start(wb_codes[:].bitcast(I32), wb_words.rearrange("a p b -> p a b").bitcast(I32))
        load_wa(0)
        nc.sync.dma_start(rows[0:4, :].rearrange("t (g i) -> t g i", i=8), ba.rearrange("(g t i) -> t g i", t=4, i=8))
        nc.sync.dma_start(rows[4:8, :].rearrange("t (g i) -> t g i", i=8), gain.rearrange("(g t i) -> t g i", t=4, i=8))
        load_wa(1)
        load_wc(0, 0, EARLY)
        load_wd(0, 0, EARLY)
        load_scale_rows(wd_sc, wd_scales)
        load_wc(1, EARLY, N)
        load_wd(1, EARLY, N)
        nc.sync.dma_start(place_list[:], offs3)
        nc.sync.dma_start(weights[:], wgo)

        def picked(words, a, j0, width):
            return words[a, j0 // HALF][:, j0 % HALF : j0 % HALF + width].bitcast(FP8X4)

        def gather_words(dst, a, lst, half, room):
            dst[a, half] = room
            nc.vector.tensor_copy(
                room,
                table[a][:].bitcast(U32).indirect(lst[:, 32 * half : 32 * (half + 1)]),
            )

        def quantise_wa_planes(a, b):
            grouped = work.tile([P, 2, P, 4], BF16, name="wa_grouped", align_bytes=64)
            for u in range(2):
                nc.vector.tensor_copy(
                    grouped[:, u].rearrange("p (g h i) j -> p g h j i", h=2, i=4),
                    wa_raw[a][:].rearrange("p j (g t h i) -> p t g h j i", t=4, h=2, i=4)[:, 2 * b + u],
                )
            nc.vector.quantize_mx(
                wa_codes[a][:, 2 * P * b : 2 * P * (b + 1)].bitcast(FP8X4),
                wa_scales[a][:, 2 * P * b : 2 * P * (b + 1)],
                grouped[:].rearrange("p u m j -> p (u m j)"),
            )

        def quantise_wc(n0, width, tag, engine_copy=nc.scalar.copy):
            s, at = (0, n0) if n0 < EARLY else (1, n0 - EARLY)
            grouped = kept("wc_grouped", [P, width, 4], BF16, tag=tag)
            engine_copy(
                grouped[:].rearrange("p (c i) t -> p c t i", i=4),
                wc_raw[s][:, :, at : at + width].rearrange("p t (c i) -> p c t i", i=4),
            )
            nc.vector.quantize_mx(
                wc_codes[:, n0 : n0 + width].bitcast(FP8X4),
                wc_scales[:, n0 : n0 + width],
                grouped[:].rearrange("p m j -> p (m j)"),
            )

        nc.vector.tensor_copy(tutor_scales[:], table_scales[:].indirect(tutor_list[:]))
        nc.scalar.dma_start(tutor_scales1[0:64, :].bitcast(I32), tutor_scales[4:68, :].bitcast(I32))
        nc.scalar.dma_start(tutor_scales1[64:100, :].bitcast(I32), tutor_scales[68:104, :].bitcast(I32))
        nc.vector.tensor_copy(pupil_scales[:], table_scales[:].indirect(pupil_list[:]))
        clear_page(3, nc.gpsimd, "table_scales")
        gather_words(tutor, 0, tutor_list, 0, kept("tutor00", [P, HALF], U32)[:])
        gather_words(pupil, 0, pupil_list, 0, kept("pupil00", [P, HALF], U32)[:])
        gather_words(tutor, 0, tutor_list, 1, kept("tutor01", [P, HALF], U32)[:])
        gather_words(pupil, 0, pupil_list, 1, kept("pupil01", [P, HALF], U32)[:])
        clear_page(4, nc.gpsimd, "table0")
        gather_words(tutor, 1, tutor_list, 0, kept("tutor10", [P, HALF], U32)[:])
        gather_words(pupil, 1, pupil_list, 0, kept("pupil10", [P, HALF], U32)[:])
        turned = psum.tile([P, BANK], F32, name="fit")
        nc.tensor.transpose(turned[:, 0:P], rows[:], identity[:])
        nc.scalar.copy(columns[:], turned[:, 0:8])

        tutor_plane = [tutor_scales[:], tutor_scales1[:]]
        pupil_plane = [pupil_scales[:], pupil_scales[4:P, :]]

        offers, fractions, turns, sines, tanhs, sums = {}, {}, {}, {}, {}, {}

        def offer_product(c, b):
            cols = slice(CHUNK * c + P * b, CHUNK * c + P * (b + 1))
            bank = psum.tile([P, BANK], F32, name="stage", bufs=4)
            for a in range(PASSES):
                nc.tensor.matmul_mx(
                    bank[:],
                    lhsT=picked(tutor, a, cols.start, P),
                    lhsT_scale=tutor_plane[a][:, cols],
                    rhs=wb_codes[:, a, :].bitcast(FP4X4),
                    rhs_scale=wb_sc[:, a, :],
                    start=(a == 0),
                    stop=(a == PASSES - 1),
                )
            by_plane = bank[:].rearrange("p (g t i) -> p t g i", t=4, i=8)
            shifted = kept("shifted", [P, H], U32, tag="phase%d" % b)
            nc.scalar.activation(
                shifted[:].rearrange("p (t g i) -> p t g i", t=4, i=8),
                by_plane,
                ACT.Silu,
                bias=MAGIC,
                scale=1.0 / (2.0 * math.pi),
            )
            offers[c, b] = (by_plane, shifted)

        def offer_turns(c, b):
            by_plane, shifted = offers[c, b]
            if b == 0:
                fractions[c] = kept("revolutions", [P, 2, H], F32, tag="sine_terms")
            revolutions = fractions[c]
            nc.scalar.activation(
                revolutions[:, b, :].rearrange("p (t g i) -> p t g i", t=4, i=8),
                by_plane,
                ACT.Copy,
                scale=1.0 / (2.0 * math.pi),
            )
            whole = work.tile([P, H], F32, name="whole")
            nc.scalar.activation(whole[:], shifted[:], ACT.Copy, bias=MAGIC, scale=-1.0)
            turns[c, b] = (revolutions[:, b, :], whole[:])

        def offer_sine(c):
            angles = [psum.tile([P, BANK], F32, name="stage", bufs=4) for b in range(2)]
            for jt in range(2):
                for t in range(4):
                    at = CHUNK * (t % 2) + P * jt
                    for term in range(2):
                        nc.tensor.matmul(
                            angles[t // 2][:, at : at + P],
                            lhsT=turns[c, jt][term][:, P * t : P * (t + 1)],
                            rhs=identity[:],
                            is_transpose=True,
                            start=(term == 0),
                            stop=(term == 1),
                        )
            plain = [kept("sine", [P, BANK], F32, tag="phase%d" % b) for b in range(2)]
            for b in range(2):
                nc.scalar.activation(plain[b][:], angles[b][:], ACT.Sin, scale=2.0 * math.pi)
            gained = kept("gained", [P, 4, CHUNK], F32, tag="sine_terms")
            for t in range(4):
                sine = plain[t // 2][:, CHUNK * (t % 2) : CHUNK * (t % 2 + 1)]
                if c == 0:
                    nc.vector.tensor_scalar(gained[:, t, :], sine, columns[:, 4 + t : 5 + t], None, ALU.mult)
                else:
                    nc.scalar.activation(gained[:, t, :], sine, ACT.Copy, scale=columns[:, 4 + t : 5 + t])
                sines[c, t] = gained[:, t, :]

        def ask_product(c):
            cols = slice(CHUNK * c, CHUNK * (c + 1))
            for b in range(2):
                bank = psum.tile([P, BANK], F32, name="stage", bufs=4)
                for u in range(2):
                    t = 2 * b + u
                    for a in range(PASSES):
                        nc.tensor.matmul_mx(
                            bank[:, CHUNK * u : CHUNK * (u + 1)],
                            lhsT=wa_codes[a][:, P * t : P * (t + 1)].bitcast(FP8X4),
                            lhsT_scale=wa_scales[a][:, P * t : P * (t + 1)],
                            rhs=picked(pupil, a, cols.start, CHUNK),
                            rhs_scale=pupil_plane[a][:, cols],
                            start=(a == 0),
                            stop=(a == PASSES - 1),
                        )
                for u in range(2):
                    t = 2 * b + u
                    ask = work.tile([P, CHUNK], F32, name="ask_sb", bufs=4)
                    nc.scalar.activation(
                        ask[:], bank[:, CHUNK * u : CHUNK * (u + 1)], ACT.Tanh, bias=columns[:, t : t + 1]
                    )
                    tanhs[c, t] = ask

        def add_up(c):
            total = kept("total", [P, 4, CHUNK], F32, tag="total")
            for t in range(4):
                nc.vector.scalar_tensor_tensor(
                    total[:, t, :], tanhs[c, t][:], columns[:, 4 + t : 5 + t], sines[c, t], ALU.mult, ALU.add
                )
            sums[c] = total

        grouped_h = {}

        def interleave_h(c, engine_copy, grouped):
            engine_copy(
                grouped[:].rearrange("p (c i) t -> p c t i", i=4), sums[c][:].rearrange("p t (c i) -> p c t i", i=4)
            )
            grouped_h[c] = grouped

        def quantise_h(c):
            cols = slice(CHUNK * c, CHUNK * (c + 1))
            nc.vector.quantize_mx(
                h_codes[:, cols].bitcast(FP8X4), h_scales[:, cols], grouped_h[c][:].rearrange("p m j -> p (m j)")
            )

        owns, maxima, scores = {}, {}, {}

        def own_product(cell, own=None):
            bank = psum.tile([P, BANK], F32, name="own")
            at = 0
            for tile, j0, width in cell:
                s, n0 = (0, P * tile) if P * tile < EARLY else (1, P * tile - EARLY)
                for a in range(PASSES):
                    nc.tensor.matmul_mx(
                        bank[:, at : at + width],
                        lhsT=wd_codes[s][:, a, n0 : n0 + P].bitcast(FP8X4),
                        lhsT_scale=wd_sc[:, a, P * tile : P * (tile + 1)],
                        rhs=picked(tutor, a, j0, width),
                        rhs_scale=tutor_plane[a][:, j0 : j0 + width],
                        start=(a == 0),
                        stop=(a == PASSES - 1),
                    )
                at += width
            if own is None:
                own = work.tile([P, BANK], F32, name="own_sb", bufs=5)
            nc.scalar.copy(own[:, 0:at], bank[:, 0:at])
            owns[cell] = own

        def score(cell):
            bank = psum.tile([P, BANK], F32, name="fit")
            at = 0
            for tile, j0, width in cell:
                nc.tensor.matmul_mx(
                    bank[:, at : at + width],
                    lhsT=wc_codes[:, P * tile : P * (tile + 1)].bitcast(FP8X4),
                    lhsT_scale=wc_scales[:, P * tile : P * (tile + 1)],
                    rhs=h_codes[:, j0 : j0 + width].bitcast(FP8X4),
                    rhs_scale=h_scales[:, j0 : j0 + width],
                    start=True,
                    stop=True,
                )
                at += width
            larger = work.tile([P, BANK], F32, name="larger", bufs=5)
            nc.vector.tensor_tensor(larger[:, 0:at], bank[:, 0:at], owns[cell][:, 0:at], ALU.max)
            maxima[cell] = larger

        def magnitude(cell, first, count, size=None):
            width = cell[0][2]
            if size is None:
                size = work.tile([P, BANK], F32, name="size", bufs=4)
            nc.scalar.activation(
                size[:, 0 : width * count], maxima[cell][:, width * first : width * (first + count)], ACT.Abs
            )
            for piece in range(count):
                scores[cell, first + piece] = size[:, width * piece : width * (piece + 1)]

        def place(cell, piece):
            tile, j0, width = cell[piece]
            page = pages[tile]
            nc.vector.tensor_tensor(
                page[:].indirect(place_list[:, j0 // 16 : (j0 + width) // 16]),
                scores[cell, piece],
                weights[:, j0 : j0 + width],
                ALU.mult,
            )
            if j0 + width == S:
                nc.sync.dma_start(out[P * tile : P * (tile + 1), :], page[:])

        def narrow(c, *tiles):
            return tuple((tile, CHUNK * c, CHUNK) for tile in tiles)

        windows = [[narrow(c, 0), narrow(c, 1, 2), narrow(c, 3, 4)] for c in range(CHUNKS)]
        closing = [((5, HALF * half, HALF),) for half in range(2)]

        for b in range(2):
            offer_product(0, b)
            offer_turns(0, b)
        for a in range(PASSES):
            for b in range(2):
                quantise_wa_planes(a, b)
        gather_words(pupil, 1, pupil_list, 1, kept("pupil11", [P, HALF], U32, tag="wa_raw1")[:])
        offer_sine(0)
        ask_product(0)
        quantise_wc(0, P, "")
        own_product(windows[0][0])
        add_up(0)
        interleave_h(0, nc.vector.tensor_copy, kept("h_grouped0", [P, CHUNK, 4], BF16, tag="first_h"))
        quantise_h(0)
        gather_words(tutor, 1, tutor_list, 1, kept("tutor11", [P, HALF], U32, tag="first_h")[:])
        quantise_wc(P, 2 * P, "phase0")
        own_product(windows[0][1])
        for c in range(CHUNKS - 1):
            first, second, third = windows[c]
            score(first)
            score(second)
            if c > 0:
                offer_turns(c + 1, 0)
            magnitude(first, 0, len(first))
            if c == 0:
                offer_product(c + 1, 0)
                offer_turns(c + 1, 0)
                quantise_wc(3 * P, 2 * P, "wc34", nc.vector.tensor_copy)
            magnitude(second, 0, len(second))
            offer_product(c + 1, 1)
            offer_turns(c + 1, 1)
            own_product(third)
            for piece in range(len(first)):
                place(first, piece)
            score(third)
            for piece in range(len(second)):
                place(second, piece)
            ask_product(c + 1)
            offer_sine(c + 1)
            add_up(c + 1)
            magnitude(third, 0, 1, kept("held_size0", [P, CHUNK], F32, tag="phase1"))
            for cell in windows[c + 1][:2]:
                own_product(cell)
            if c + 2 < CHUNKS:
                offer_product(c + 2, 0)
            else:
                own_product(windows[c + 1][2])
            interleave_h(c + 1, nc.scalar.copy, kept("h_grouped", [P, CHUNK, 4], BF16))
            place(third, 0)
            quantise_h(c + 1)
            magnitude(third, 1, 1)
            place(third, 1)
        quantise_wc(5 * P, P, "")
        for cell in closing:
            own_product(cell)
        for cell in windows[-1]:
            score(cell)
            magnitude(cell, 0, len(cell))
        closing_size = kept("closing_size", [P, S], F32)
        for half, cell in enumerate(closing):
            score(cell)
            magnitude(cell, 0, 1, closing_size[:, HALF * half : HALF * (half + 1)])
        for cell in windows[-1]:
            for piece in range(len(cell)):
                place(cell, piece)
        nc.vector.tensor_tensor(pages[0][:].indirect(place_list[:]), closing_size[:], weights[:], ALU.mult)
        nc.sync.dma_start(out[P * RESIDENT :, :], pages[0][:])
